import numpy as np
CORES = [0,4,8,12,16,20,24,28,32,36,40,44,48,52,56,60]
N = 16
T = 8
ROUTE = [[[8,13,15,2],[9,10,0,2],[15,0,3,9],[3,9,1,2],[4,8,6,13],[2,13,4,1],[1,5,10,8],[11,10,3,13]],[[2,0,10,12],[8,1,15,11],[6,11,4,0],[7,15,13,9],[6,13,12,4],[14,2,12,1],[0,9,10,5],[5,0,8,1]],[[12,3,0,11],[8,14,6,10],[8,7,15,0],[4,0,8,15],[3,5,6,2],[2,4,12,5],[2,14,12,8],[12,5,0,2]],[[10,13,7,11],[14,6,12,0],[13,1,14,7],[7,1,2,11],[9,10,14,12],[1,12,14,7],[12,1,2,11],[8,2,4,12]],[[10,7,0,13],[10,4,2,13],[3,4,7,2],[0,4,9,8],[4,10,12,8],[12,7,0,6],[3,1,15,13],[10,14,8,0]],[[13,11,4,15],[9,7,3,5],[14,3,2,13],[11,6,10,4],[13,3,15,4],[13,6,12,5],[8,0,11,1],[3,7,15,14]],[[11,4,1,10],[9,6,5,1],[9,15,5,10],[9,13,3,5],[5,3,12,8],[9,3,5,13],[11,4,14,12],[12,4,15,3]],[[8,3,2,9],[8,2,4,0],[5,9,0,1],[2,0,13,7],[14,13,5,8],[11,15,1,9],[6,13,14,15],[3,5,14,10]],[[11,6,10,12],[6,9,7,4],[4,0,14,8],[15,11,8,3],[2,6,11,10],[14,8,7,5],[13,7,6,4],[9,8,11,0]],[[15,0,5,14],[0,10,6,8],[2,7,15,6],[14,7,9,5],[7,5,15,4],[7,9,15,14],[12,9,13,7],[12,8,0,14]],[[15,1,7,10],[15,13,5,11],[13,10,7,0],[13,7,12,3],[0,6,8,12],[11,14,7,9],[15,8,6,4],[11,7,3,8]],[[10,0,4,14],[9,4,3,14],[15,3,8,7],[0,10,7,2],[4,1,12,11],[4,12,2,5],[12,2,5,14],[10,11,15,12]],[[5,10,8,0],[5,0,15,9],[7,10,6,0],[14,1,11,0],[3,9,6,10],[10,11,8,12],[6,1,15,0],[6,10,1,3]],[[7,14,1,4],[7,4,10,13],[2,4,7,11],[10,3,5,15],[6,5,14,7],[4,6,1,10],[12,15,5,8],[15,4,14,7]],[[8,4,3,12],[3,14,1,12],[1,2,7,0],[0,7,14,1],[6,7,0,11],[9,0,7,8],[12,5,6,14],[12,0,4,7]],[[8,14,11,2],[15,2,1,8],[4,6,1,12],[13,3,8,6],[1,6,14,10],[7,6,12,10],[13,14,5,2],[5,7,13,2]]]
YW = 40
def setup_inputs(rng):
    return {"x": rng.standard_normal((N, 128, T), dtype=np.float32)}
def reference(x):
    y = np.full((N, 128, YW), np.nan, x.dtype)
    fill = [0] * N
    for r in range(N):
        for t in range(T):
            for e in ROUTE[r][t]:
                y[e][:, fill[e]] = x[r][:, t]
                fill[e] += 1
    return {"y": y}

@@ -1,0 +1,79 @@
+from concourse import bass
+
+SCRATCH = {
+    "xs": ("sbuf", [128, 8], "float32"),
+    "land": ("sbuf", [128, 40], "float32"),
+}
+SEMAPHORES = ["loaded", "got", "done", "stored"]
+
+
+def plan(tables, cores, topo):
+    route = tables["ROUTE"]
+    n = len(cores)
+    pos = {}
+    fill = [0] * n
+    for r in range(n):
+        for t in range(len(route[r])):
+            for e in route[r][t]:
+                pos[(r, t, e)] = fill[e]
+                fill[e] += 1
+    calls = {}
+    for r in range(n):
+        c = cores[r]
+        par = topo.chip(c) & 1
+        for t in range(len(route[r])):
+            far = [(cores[e], pos[(r, t, e)]) for e in route[r][t] if (topo.chip(cores[e]) & 1) != par]
+            near = [(cores[e], pos[(r, t, e)]) for e in route[r][t] if (topo.chip(cores[e]) & 1) == par and e != r]
+            own = [(c, pos[(r, t, e)]) for e in route[r][t] if e == r]
+            pair = 3 << (2 * (t % 4))
+            if far:
+                calls.setdefault(c + 2 + t // 4, []).append((t, 1, far, pair))
+            if near:
+                calls.setdefault(c + t // 4, []).append((t, 1, near, pair))
+            if own:
+                calls.setdefault(c + 1, []).append((t, 1, own, 1 << (8 + t)))
+    return calls, fill
+
+
+def ones(mask):
+    return bin(mask).count("1")
+
+
+def rank_program(g, core, T, topo):
+    calls, fill = plan(T.tables, T.cores, topo)
+    rank = T.rank_of(core)
+    mine = calls.get(core, [])
+
+    def send(local_sem):
+        trs = []
+        for (t0, w, dsts, mask) in mine:
+            ids = [bass.DstId(rid=topo.addr(d)[0], pnc=topo.addr(d)[1]) for d, p in dsts]
+            trs.append(bass.RemoteDMATransfer(dst_ids=ids, dma_engine_mask=mask, remote_sem=T.sem.done,
+                                              srcs=[T.xs[:, t0:t0 + w]], dsts=[T.land[:, p:p + w] for d, p in dsts]))
+        if trs:
+            g.remote_dma_fused(trs, local_sem=local_sem)
+        return sum(ones(m) for (t0, w, dsts, m) in mine)
+
+    if rank is None:
+        if core % 4 == 0 or not mine:
+            return
+        g.wait_ge(T.sem.got, 16)
+        left = send(T.sem.done)
+        g.wait_ge(T.sem.done, left)
+        return
+
+    g.dma_start(out=T.xs[:, :], in_=T.x[:, :]).then_inc(T.sem.loaded, 16)
+    g.wait_ge(T.sem.loaded, 16)
+    helpers = [h for h in (core + 1, core + 2, core + 3) if calls.get(h)]
+    ids = [bass.DstId(rid=topo.addr(h)[0], pnc=topo.addr(h)[1]) for h in helpers]
+    g.remote_dma_fused([bass.RemoteDMATransfer(dst_ids=ids, dma_engine_mask=0xFFFF, remote_sem=T.sem.got,
+                                               srcs=[T.xs[:, :]], dsts=[T.xs[:, :] for h in helpers])],
+                       local_sem=T.sem.done)
+    total = 16 + send(T.sem.done)
+    for trs in calls.values():
+        for (t0, w, dsts, mask) in trs:
+            total += sum(ones(mask) for d, p in dsts if d == core)
+    g.wait_ge(T.sem.done, total)
+    k = fill[rank]
+    g.dma_start(out=T.y[:, 0:k], in_=T.land[:, 0:k]).then_inc(T.sem.stored, 16)
+    g.wait_ge(T.sem.stored, 16)

@@ -1,78 +1,196 @@
 from concourse import bass
 
 SCRATCH = {
-    "xs": ("sbuf", [128, 8], "float32"),
+    "xs": ("sbuf", [128, 16], "float32"),
     "land": ("sbuf", [128, 40], "float32"),
 }
 SEMAPHORES = ["loaded", "got", "done", "stored"]
-
-
-def plan(tables, cores, topo):
-    route = tables["ROUTE"]
-    n = len(cores)
-    pos = {}
-    fill = [0] * n
-    for r in range(n):
-        for t in range(len(route[r])):
-            for e in route[r][t]:
-                pos[(r, t, e)] = fill[e]
-                fill[e] += 1
-    calls = {}
-    for r in range(n):
-        c = cores[r]
-        par = topo.chip(c) & 1
-        for t in range(len(route[r])):
-            far = [(cores[e], pos[(r, t, e)]) for e in route[r][t] if (topo.chip(cores[e]) & 1) != par]
-            near = [(cores[e], pos[(r, t, e)]) for e in route[r][t] if (topo.chip(cores[e]) & 1) == par and e != r]
-            own = [(c, pos[(r, t, e)]) for e in route[r][t] if e == r]
-            pair = 3 << (2 * (t % 4))
-            if far:
-                calls.setdefault(c + 2 + t // 4, []).append((t, 1, far, pair))
-            if near:
-                calls.setdefault(c + t // 4, []).append((t, 1, near, pair))
-            if own:
-                calls.setdefault(c + 1, []).append((t, 1, own, 1 << (8 + t)))
-    return calls, fill
 
 
 def ones(mask):
     return bin(mask).count("1")
 
 
-def rank_program(g, core, T, topo):
-    calls, fill = plan(T.tables, T.cores, topo)
-    rank = T.rank_of(core)
-    mine = calls.get(core, [])
+def configs(n):
+    out = [[]]
+    for i in range(n):
+        out = [c + [w] for c in out for w in (1, 2)]
+    return out
 
-    def send(local_sem):
-        trs = []
-        for (t0, w, dsts, mask) in mine:
-            ids = [bass.DstId(rid=topo.addr(d)[0], pnc=topo.addr(d)[1]) for d, p in dsts]
-            trs.append(bass.RemoteDMATransfer(dst_ids=ids, dma_engine_mask=mask, remote_sem=T.sem.done,
-                                              srcs=[T.xs[:, t0:t0 + w]], dsts=[T.land[:, p:p + w] for d, p in dsts]))
-        if trs:
-            g.remote_dma_fused(trs, local_sem=local_sem)
-        return sum(ones(m) for (t0, w, dsts, m) in mine)
+
+def split(u):
+    r, t0, w, e = u
+    return [(r, t0, 1, e), (r, t0 + 1, 1, e)]
+
+
+def place(units, cores, home, cap=8):
+    best = None
+    for cfg in configs(len(cores)):
+        u = {1: [x for x in units if x[2] == 1], 2: [x for x in units if x[2] == 2]}
+        room2 = cap * cfg.count(2)
+        while len(u[2]) > room2:
+            u[1] += split(u[2].pop())
+        load = {c: [[], []] for c in cores}
+        cross = set()
+        left = []
+        for w in (2, 1):
+            cw = [c for c, k in zip(cores, cfg) if k == w]
+            rest = []
+            for r in sorted(set(x[0] for x in u[w])):
+                mine = [x for x in u[w] if x[0] == r]
+                hs = [c for c in cw if c in home[r]]
+                for x in mine:
+                    hs.sort(key=lambda c: len(load[c][0]))
+                    if hs and len(load[hs[0]][0]) < cap:
+                        load[hs[0]][0].append(x)
+                    else:
+                        rest.append(x)
+            for x in rest:
+                cs = sorted(cw, key=lambda c: ((x[0], c) not in cross and c not in home[x[0]], len(load[c][0])))
+                cs = [c for c in cs if len(load[c][0]) < cap]
+                if cs:
+                    load[cs[0]][0].append(x)
+                    if cs[0] not in home[x[0]]:
+                        cross.add((x[0], cs[0]))
+                else:
+                    left.append(x)
+        for x in left:
+            cs = sorted(cores, key=lambda c: (c not in home[x[0]] and (x[0], c) not in cross,
+                                              len(load[c][0]) + len(load[c][1])))
+            cs = [c for c in cs if len(load[c][0]) + len(load[c][1]) < cap and
+                  (not load[c][1] or load[c][1][0][2] == x[2])]
+            if not cs:
+                load = None
+                break
+            load[cs[0]][1].append(x)
+            if cs[0] not in home[x[0]]:
+                cross.add((x[0], cs[0]))
+        if load is None:
+            continue
+        nw = sum(len(a) + len(b) for a, b in load.values())
+        peak = max(len(a) + len(b) for a, b in load.values())
+        cost = (len(left) > 0, len(left), len(cross), nw, peak)
+        if best is None or cost < best[0]:
+            best = (cost, load)
+    return best[1]
+
+
+def engines(n, first, cap=8):
+    size = [1] * n
+    while True:
+        i = min(range(n), key=lambda k: size[k]) if n else None
+        if i is None or sum(size) + size[i] > cap:
+            break
+        size[i] *= 2
+    masks, at = [], first
+    for s in size:
+        masks.append(((1 << s) - 1) << at)
+        at += s
+    return masks
+
+
+def plan(tables, cores, topo):
+    route = tables["ROUTE"]
+    n = len(cores)
+    pos, fill = {}, [0] * n
+    for r in range(n):
+        for t in range(len(route[r])):
+            for e in route[r][t]:
+                pos[(r, t, e)] = fill[e]
+                fill[e] += 1
+    units = []
+    for r in range(n):
+        for e in range(n):
+            ts = [t for t in range(len(route[r])) if e in route[r][t]]
+            i = 0
+            while i < len(ts):
+                if i + 1 < len(ts) and ts[i + 1] == ts[i] + 1:
+                    units.append((r, ts[i], 2, e))
+                    i += 2
+                else:
+                    units.append((r, ts[i], 1, e))
+                    i += 1
+    chip = lambda r: topo.chip(cores[r])
+    jobs = {}
+    for ch in sorted(set(chip(r) for r in range(n))):
+        rs = [r for r in range(n) if chip(r) == ch]
+        far = [u for u in units if u[0] in rs and (chip(u[3]) & 1) != (ch & 1)]
+        ports = [c for c in range(ch * 8, ch * 8 + 8) if c % 4 >= 2]
+        home = {r: [c for c in ports if topo.die(c) == topo.die(cores[r])] for r in rs}
+        jobs.update(place(far, ports, home))
+        for r in rs:
+            near = [u for u in units if u[0] == r and chip(u[3]) != ch and (chip(u[3]) & 1) == (ch & 1)]
+            pair = [cores[r], cores[r] + 1]
+            jobs.update(place(near, pair, {r: pair}))
+    local = {c: [[], []] for c in jobs}
+    holds = lambda c, r: c == cores[r] or any(u[0] == r for call in jobs[c] for u in call)
+    todo = [u for u in units if chip(u[3]) == chip(u[0])]
+    while todo:
+        u = todo.pop()
+        r, t0, w, e = u
+        cs = []
+        for c in jobs:
+            if topo.chip(c) != chip(r) or c == cores[e] or not holds(c, r):
+                continue
+            for k in (0, 1):
+                if jobs[c][k] and jobs[c][k][0][2] == w and len(local[c][0]) + len(local[c][1]) < 8:
+                    cs.append((len(local[c][0]) + len(local[c][1]), k, c != cores[r], c))
+        if cs:
+            m, k, x, c = min(cs)
+            local[c][k].append(u)
+        else:
+            todo += split(u)
+    calls, feeds = {}, {cores[r]: [] for r in range(n)}
+    for c in jobs:
+        off = engines(len(jobs[c][0]) + len(jobs[c][1]), 0)
+        on = engines(len(local[c][0]) + len(local[c][1]), 8)
+        calls[c] = []
+        for k in (0, 1):
+            trs = []
+            for lst, masks in ((jobs[c][k], off), (local[c][k], on)):
+                for (r, t0, w, e) in lst:
+                    trs.append(((cores[r] % 8) * 2 + t0, w, cores[e], pos[(r, t0, e)], masks.pop(0)))
+                    if c != cores[r] and c not in feeds[cores[r]]:
+                        feeds[cores[r]].append(c)
+            if trs:
+                calls[c].append(trs)
+    return calls, feeds, fill
+
+
+def rank_program(g, core, T, topo):
+    calls, feeds, fill = plan(T.tables, T.cores, topo)
+    rank = T.rank_of(core)
+
+    def dst(c):
+        return bass.DstId(rid=topo.addr(c)[0], pnc=topo.addr(c)[1])
+
+    def send():
+        left = 0
+        for trs in calls.get(core, []):
+            g.remote_dma_fused([bass.RemoteDMATransfer(dst_ids=[dst(d)], dma_engine_mask=m, remote_sem=T.sem.done,
+                                                       srcs=[T.xs[:, a:a + w]], dsts=[T.land[:, p:p + w]])
+                                for (a, w, d, p, m) in trs], local_sem=T.sem.done)
+            left += sum(ones(m) for (a, w, d, p, m) in trs)
+        return left
 
     if rank is None:
-        if core % 4 == 0 or not mine:
-            return
-        g.wait_ge(T.sem.got, 16)
-        left = send(T.sem.done)
-        g.wait_ge(T.sem.done, left)
+        fed = sum(core in hs for hs in feeds.values())
+        if fed:
+            g.wait_ge(T.sem.got, 16 * fed)
+            g.wait_ge(T.sem.done, send())
         return
 
-    g.dma_start(out=T.xs[:, :], in_=T.x[:, :]).then_inc(T.sem.loaded, 16)
+    a = (core % 8) * 2
+    g.dma_start(out=T.xs[:, a:a + 8], in_=T.x[:, :]).then_inc(T.sem.loaded, 16)
     g.wait_ge(T.sem.loaded, 16)
-    helpers = [h for h in (core + 1, core + 2, core + 3) if calls.get(h)]
-    ids = [bass.DstId(rid=topo.addr(h)[0], pnc=topo.addr(h)[1]) for h in helpers]
-    g.remote_dma_fused([bass.RemoteDMATransfer(dst_ids=ids, dma_engine_mask=0xFFFF, remote_sem=T.sem.got,
-                                               srcs=[T.xs[:, :]], dsts=[T.xs[:, :] for h in helpers])],
-                       local_sem=T.sem.done)
-    total = 16 + send(T.sem.done)
-    for trs in calls.values():
-        for (t0, w, dsts, mask) in trs:
-            total += sum(ones(mask) for d, p in dsts if d == core)
+    hs = feeds[core]
+    g.remote_dma_fused([bass.RemoteDMATransfer(dst_ids=[dst(h) for h in hs], dma_engine_mask=0xFFFF,
+                                               remote_sem=T.sem.got, srcs=[T.xs[:, a:a + 8]],
+                                               dsts=[T.xs[:, a:a + 8] for h in hs])], local_sem=T.sem.done)
+    total = 16 + send()
+    for cl in calls.values():
+        for trs in cl:
+            total += sum(ones(m) for (a2, w, d, p, m) in trs if d == core)
     g.wait_ge(T.sem.done, total)
     k = fill[rank]
     g.dma_start(out=T.y[:, 0:k], in_=T.land[:, 0:k]).then_inc(T.sem.stored, 16)

@@ -23,65 +23,103 @@ def split(u):
     return [(r, t0, 1, e), (r, t0 + 1, 1, e)]
 
 
-def place(units, cores, home, cap=8):
+def groups(lst):
+    by = {}
+    for u in lst:
+        by.setdefault(u[:3], []).append(u)
+    out = []
+    for k in sorted(by):
+        us = by[k]
+        while us:
+            n = 4 if len(us) >= 4 else 2 if len(us) >= 2 else 1
+            out.append(us[:n])
+            us = us[n:]
+    return out
+
+
+def place_far(units, cores, home, near_mate, cap=8):
     best = None
     for cfg in configs(len(cores)):
-        u = {1: [x for x in units if x[2] == 1], 2: [x for x in units if x[2] == 2]}
-        room2 = cap * cfg.count(2)
-        while len(u[2]) > room2:
-            u[1] += split(u[2].pop())
-        load = {c: [[], []] for c in cores}
-        cross = set()
-        left = []
-        for w in (2, 1):
-            cw = [c for c, k in zip(cores, cfg) if k == w]
-            rest = []
-            for r in sorted(set(x[0] for x in u[w])):
-                mine = [x for x in u[w] if x[0] == r]
-                hs = [c for c in cw if c in home[r]]
-                for x in mine:
-                    hs.sort(key=lambda c: len(load[c][0]))
-                    if hs and len(load[hs[0]][0]) < cap:
-                        load[hs[0]][0].append(x)
+        for even in (True, False):
+            u = {1: [x for x in units if x[2] == 1], 2: [x for x in units if x[2] == 2]}
+            while len(u[2]) > cap * cfg.count(2):
+                u[1] += split(u[2].pop())
+            u[1].sort()
+            over = len(u[1]) - cap * cfg.count(1)
+            left = []
+            if over > 0:
+                left = [x for x in u[1] if near_mate(x)][-over:]
+                if len(left) < over:
+                    continue
+                u[1] = [x for x in u[1] if x not in left]
+            load = {c: [[], []] for c in cores}
+            cross = set()
+            used = lambda c: len(load[c][0]) + len(load[c][1])
+            for w in (2, 1):
+                cw = [c for c, k in zip(cores, cfg) if k == w]
+                rest = []
+                for gr in groups(u[w]):
+                    hs = [c for c in cw if c in home[gr[0][0]] and used(c) + len(gr) <= cap]
+                    if hs:
+                        load[min(hs, key=used) if even else hs[0]][0] += gr
                     else:
-                        rest.append(x)
-            for x in rest:
-                cs = sorted(cw, key=lambda c: ((x[0], c) not in cross and c not in home[x[0]], len(load[c][0])))
-                cs = [c for c in cs if len(load[c][0]) < cap]
-                if cs:
-                    load[cs[0]][0].append(x)
-                    if cs[0] not in home[x[0]]:
-                        cross.add((x[0], cs[0]))
-                else:
-                    left.append(x)
-        for x in left:
-            cs = sorted(cores, key=lambda c: (c not in home[x[0]] and (x[0], c) not in cross,
-                                              len(load[c][0]) + len(load[c][1])))
-            cs = [c for c in cs if len(load[c][0]) + len(load[c][1]) < cap and
-                  (not load[c][1] or load[c][1][0][2] == x[2])]
-            if not cs:
-                load = None
-                break
-            load[cs[0]][1].append(x)
-            if cs[0] not in home[x[0]]:
-                cross.add((x[0], cs[0]))
-        if load is None:
-            continue
-        nw = sum(len(a) + len(b) for a, b in load.values())
-        peak = max(len(a) + len(b) for a, b in load.values())
-        cost = (len(left) > 0, len(left), len(cross), nw, peak)
-        if best is None or cost < best[0]:
-            best = (cost, load)
+                        rest += gr
+                for x in rest:
+                    cs = [c for c in cw if used(c) < cap]
+                    c = min(cs, key=lambda c: (c not in home[x[0]] and (x[0], c) not in cross, used(c)))
+                    load[c][0].append(x)
+                    if c not in home[x[0]]:
+                        cross.add((x[0], c))
+            for x in left:
+                cs = [c for c in cores if used(c) < cap and load[c][0] and load[c][0][0][2] != 1]
+                if not cs:
+                    load = None
+                    break
+                c = min(cs, key=lambda c: (c not in home[x[0]] and (x[0], c) not in cross, not load[c][1], used(c)))
+                load[c][1].append(x)
+                if c not in home[x[0]]:
+                    cross.add((x[0], c))
+            if load is None:
+                continue
+            fan = max([sum(1 for p in cross if p[0] == r) for r in home])
+            most = max(len(groups(a)) + len(groups(b)) for a, b in load.values())
+            cost = (len(left), fan, len(cross), most, sum(used(c) for c in cores))
+            if best is None or cost < best[0]:
+                best = (cost, load)
     return best[1]
 
 
-def engines(n, first, cap=8):
-    size = [1] * n
-    while True:
-        i = min(range(n), key=lambda k: size[k]) if n else None
-        if i is None or sum(size) + size[i] > cap:
+def place_near(off, on, c, h, cores):
+    best = None
+    for cfg in configs(2):
+        width = {c: cfg[0], h: cfg[1]}
+        out, stay, ok = {c: [], h: []}, {c: [], h: []}, True
+        for todo, load in ((sorted(off, key=lambda x: x[2]), out), (sorted(on, key=lambda x: x[2]), stay)):
+            while todo and ok:
+                x = todo.pop()
+                cs = [k for k in (c, h) if width[k] == x[2] and len(load[k]) < 8 and k != cores[x[3]]]
+                if cs:
+                    load[min(cs, key=lambda k: len(load[k]))].append(x)
+                elif x[2] == 2:
+                    todo = split(x) + todo
+                else:
+                    ok = False
+        cost = sum(len(v) for v in out.values()) + sum(len(v) for v in stay.values())
+        if ok and (best is None or cost < best[0]):
+            best = (cost, out, stay)
+    return best[1], best[2]
+
+
+def engines(sizes, first, cap=8):
+    size = list(sizes)
+    mult = [1] * len(size)
+    while size:
+        fit = [i for i in range(len(size)) if sum(size) + size[i] <= cap]
+        if not fit:
             break
+        i = min(fit, key=lambda k: mult[k])
         size[i] *= 2
+        mult[i] *= 2
     masks, at = [], first
     for s in size:
         masks.append(((1 << s) - 1) << at)
@@ -104,56 +142,42 @@ def plan(tables, cores, topo):
             ts = [t for t in range(len(route[r])) if e in route[r][t]]
             i = 0
             while i < len(ts):
-                if i + 1 < len(ts) and ts[i + 1] == ts[i] + 1:
-                    units.append((r, ts[i], 2, e))
-                    i += 2
-                else:
-                    units.append((r, ts[i], 1, e))
-                    i += 1
+                w = 2 if i + 1 < len(ts) and ts[i + 1] == ts[i] + 1 else 1
+                units.append((r, ts[i], w, e))
+                i += w
     chip = lambda r: topo.chip(cores[r])
-    jobs = {}
+    work = {}
     for ch in sorted(set(chip(r) for r in range(n))):
         rs = [r for r in range(n) if chip(r) == ch]
         far = [u for u in units if u[0] in rs and (chip(u[3]) & 1) != (ch & 1)]
         ports = [c for c in range(ch * 8, ch * 8 + 8) if c % 4 >= 2]
         home = {r: [c for c in ports if topo.die(c) == topo.die(cores[r])] for r in rs}
-        jobs.update(place(far, ports, home))
+        for c, (one, two) in place_far(far, ports, home, lambda u: topo.mates(ch, chip(u[3]))).items():
+            work[c] = [(one, []), (two, [])]
         for r in rs:
-            near = [u for u in units if u[0] == r and chip(u[3]) != ch and (chip(u[3]) & 1) == (ch & 1)]
-            pair = [cores[r], cores[r] + 1]
-            jobs.update(place(near, pair, {r: pair}))
-    local = {c: [[], []] for c in jobs}
-    holds = lambda c, r: c == cores[r] or any(u[0] == r for call in jobs[c] for u in call)
-    todo = [u for u in units if chip(u[3]) == chip(u[0])]
-    while todo:
-        u = todo.pop()
-        r, t0, w, e = u
-        cs = []
-        for c in jobs:
-            if topo.chip(c) != chip(r) or c == cores[e] or not holds(c, r):
-                continue
-            for k in (0, 1):
-                if jobs[c][k] and jobs[c][k][0][2] == w and len(local[c][0]) + len(local[c][1]) < 8:
-                    cs.append((len(local[c][0]) + len(local[c][1]), k, c != cores[r], c))
-        if cs:
-            m, k, x, c = min(cs)
-            local[c][k].append(u)
-        else:
-            todo += split(u)
+            off = [u for u in units if u[0] == r and chip(u[3]) != ch and (chip(u[3]) & 1) == (ch & 1)]
+            on = [u for u in units if u[0] == r and chip(u[3]) == ch]
+            out, stay = place_near(off, on, cores[r], cores[r] + 1, cores)
+            for c in out:
+                work[c] = [(out[c], stay[c])]
     calls, feeds = {}, {cores[r]: [] for r in range(n)}
-    for c in jobs:
-        off = engines(len(jobs[c][0]) + len(jobs[c][1]), 0)
-        on = engines(len(local[c][0]) + len(local[c][1]), 8)
-        calls[c] = []
-        for k in (0, 1):
+    for c, cl in work.items():
+        late = [(groups(a), groups(b)) for a, b in reversed(cl)]
+        off = engines([len(gr) for a, b in late for gr in a], 0)
+        on = engines([len(gr) for a, b in late for gr in b], 8)
+        got = []
+        for a, b in late:
             trs = []
-            for lst, masks in ((jobs[c][k], off), (local[c][k], on)):
-                for (r, t0, w, e) in lst:
-                    trs.append(((cores[r] % 8) * 2 + t0, w, cores[e], pos[(r, t0, e)], masks.pop(0)))
+            for lst, masks in ((a, off), (b, on)):
+                for gr in lst:
+                    r, t0, w, e = gr[0]
+                    trs.append(((cores[r] % 8) * 2 + t0, w, [(cores[u[3]], pos[(r, t0, u[3])]) for u in gr],
+                                masks.pop(0)))
                     if c != cores[r] and c not in feeds[cores[r]]:
                         feeds[cores[r]].append(c)
             if trs:
-                calls[c].append(trs)
+                got.insert(0, trs)
+        calls[c] = got
     return calls, feeds, fill
 
 
@@ -167,10 +191,11 @@ def rank_program(g, core, T, topo):
     def send():
         left = 0
         for trs in calls.get(core, []):
-            g.remote_dma_fused([bass.RemoteDMATransfer(dst_ids=[dst(d)], dma_engine_mask=m, remote_sem=T.sem.done,
-                                                       srcs=[T.xs[:, a:a + w]], dsts=[T.land[:, p:p + w]])
-                                for (a, w, d, p, m) in trs], local_sem=T.sem.done)
-            left += sum(ones(m) for (a, w, d, p, m) in trs)
+            g.remote_dma_fused([bass.RemoteDMATransfer(dst_ids=[dst(d) for d, p in ds], dma_engine_mask=m,
+                                                       remote_sem=T.sem.done, srcs=[T.xs[:, a:a + w]],
+                                                       dsts=[T.land[:, p:p + w] for d, p in ds])
+                                for (a, w, ds, m) in trs], local_sem=T.sem.done)
+            left += sum(ones(m) for (a, w, ds, m) in trs)
         return left
 
     if rank is None:
@@ -190,7 +215,7 @@ def rank_program(g, core, T, topo):
     total = 16 + send()
     for cl in calls.values():
         for trs in cl:
-            total += sum(ones(m) for (a2, w, d, p, m) in trs if d == core)
+            total += sum(ones(m) for (a2, w, ds, m) in trs for d, p in ds if d == core)
     g.wait_ge(T.sem.done, total)
     k = fill[rank]
     g.dma_start(out=T.y[:, 0:k], in_=T.land[:, 0:k]).then_inc(T.sem.stored, 16)

@@ -5,6 +5,7 @@ SCRATCH = {
     "land": ("sbuf", [128, 40], "float32"),
 }
 SEMAPHORES = ["loaded", "got", "done", "stored"]
+CALL, TRANSFER, LINK = 24, 12, 24
 
 
 def ones(mask):
@@ -110,21 +111,43 @@ def place_near(off, on, c, h, cores):
     return best[1], best[2]
 
 
-def engines(sizes, first, cap=8):
-    size = list(sizes)
-    mult = [1] * len(size)
-    while size:
-        fit = [i for i in range(len(size)) if sum(size) + size[i] <= cap]
-        if not fit:
+def schedule(cl, links):
+    items = []
+    for i, pools in enumerate(cl):
+        for pool in (0, 1):
+            items += [[i, gr, pool, len(gr)] for gr in groups(pools[pool])]
+    ahead = lambda it: 128 * len(it[1]) // it[3] + LINK * max(links(u) for u in it[1])
+    order = lambda i: sorted([it for it in items if it[0] == i], key=lambda it: -ahead(it))
+
+    def score():
+        t, worst, total = 0, 0, 0
+        for i in range(len(cl)):
+            for k, it in enumerate(order(i)):
+                t += TRANSFER + (CALL if k == 0 else 0)
+                worst = max(worst, t + ahead(it))
+                total += t + ahead(it)
+        return worst, total
+
+    while True:
+        tries = []
+        for k, it in enumerate(items):
+            if sum(o[3] for o in items if o[2] == it[2]) + it[3] <= 8:
+                it[3] *= 2
+                tries.append((score(), k))
+                it[3] //= 2
+        if not tries:
             break
-        i = min(fit, key=lambda k: mult[k])
-        size[i] *= 2
-        mult[i] *= 2
-    masks, at = [], first
-    for s in size:
-        masks.append(((1 << s) - 1) << at)
-        at += s
-    return masks
+        items[min(tries)[1]][3] *= 2
+    at = [0, 8]
+    out = []
+    for i in range(len(cl)):
+        trs = []
+        for it in order(i):
+            trs.append((it[1], ((1 << it[3]) - 1) << at[it[2]]))
+            at[it[2]] += it[3]
+        if trs:
+            out.append(trs)
+    return out
 
 
 def plan(tables, cores, topo):
@@ -160,24 +183,21 @@ def plan(tables, cores, topo):
             out, stay = place_near(off, on, cores[r], cores[r] + 1, cores)
             for c in out:
                 work[c] = [(out[c], stay[c])]
+
+    def links(u):
+        a, b = chip(u[0]), chip(u[3])
+        return 0 if a == b else 1 if topo.mates(a, b) or topo.same_plane(a, b) else 2
+
     calls, feeds = {}, {cores[r]: [] for r in range(n)}
     for c, cl in work.items():
-        late = [(groups(a), groups(b)) for a, b in reversed(cl)]
-        off = engines([len(gr) for a, b in late for gr in a], 0)
-        on = engines([len(gr) for a, b in late for gr in b], 8)
-        got = []
-        for a, b in late:
-            trs = []
-            for lst, masks in ((a, off), (b, on)):
-                for gr in lst:
-                    r, t0, w, e = gr[0]
-                    trs.append(((cores[r] % 8) * 2 + t0, w, [(cores[u[3]], pos[(r, t0, u[3])]) for u in gr],
-                                masks.pop(0)))
-                    if c != cores[r] and c not in feeds[cores[r]]:
-                        feeds[cores[r]].append(c)
-            if trs:
-                got.insert(0, trs)
-        calls[c] = got
+        calls[c] = []
+        for trs in schedule(cl, links):
+            calls[c].append([((cores[gr[0][0]] % 8) * 2 + gr[0][1], gr[0][2],
+                              [(cores[u[3]], pos[(u[0], u[1], u[3])]) for u in gr], m) for gr, m in trs])
+            for gr, m in trs:
+                src = cores[gr[0][0]]
+                if c != src and c not in feeds[src]:
+                    feeds[src].append(c)
     return calls, feeds, fill
 
 
@@ -208,7 +228,7 @@ def rank_program(g, core, T, topo):
     a = (core % 8) * 2
     g.dma_start(out=T.xs[:, a:a + 8], in_=T.x[:, :]).then_inc(T.sem.loaded, 16)
     g.wait_ge(T.sem.loaded, 16)
-    hs = feeds[core]
+    hs = sorted(feeds[core], key=lambda h: h % 4 < 2)
     g.remote_dma_fused([bass.RemoteDMATransfer(dst_ids=[dst(h) for h in hs], dma_engine_mask=0xFFFF,
                                                remote_sem=T.sem.got, srcs=[T.xs[:, a:a + 8]],
                                                dsts=[T.xs[:, a:a + 8] for h in hs])], local_sem=T.sem.done)

from concourse import bass

SCRATCH = {
    "xs": ("sbuf", [128, 16], "float32"),
    "land": ("sbuf", [128, 40], "float32"),
}
SEMAPHORES = ["loaded", "got", "done", "stored"]
CALL, TRANSFER, LINK = 24, 12, 24


def ones(mask):
    return bin(mask).count("1")


def configs(n):
    out = [[]]
    for i in range(n):
        out = [c + [w] for c in out for w in (1, 2)]
    return out


def split(u):
    r, t0, w, e = u
    return [(r, t0, 1, e), (r, t0 + 1, 1, e)]


def groups(lst):
    by = {}
    for u in lst:
        by.setdefault(u[:3], []).append(u)
    out = []
    for k in sorted(by):
        us = by[k]
        while us:
            n = 4 if len(us) >= 4 else 2 if len(us) >= 2 else 1
            out.append(us[:n])
            us = us[n:]
    return out


def place_far(units, cores, home, near_mate, cap=8):
    best = None
    for cfg in configs(len(cores)):
        for even in (True, False):
            u = {1: [x for x in units if x[2] == 1], 2: [x for x in units if x[2] == 2]}
            while len(u[2]) > cap * cfg.count(2):
                u[1] += split(u[2].pop())
            u[1].sort()
            over = len(u[1]) - cap * cfg.count(1)
            left = []
            if over > 0:
                left = [x for x in u[1] if near_mate(x)][-over:]
                if len(left) < over:
                    continue
                u[1] = [x for x in u[1] if x not in left]
            load = {c: [[], []] for c in cores}
            cross = set()
            used = lambda c: len(load[c][0]) + len(load[c][1])
            for w in (2, 1):
                cw = [c for c, k in zip(cores, cfg) if k == w]
                rest = []
                for gr in groups(u[w]):
                    hs = [c for c in cw if c in home[gr[0][0]] and used(c) + len(gr) <= cap]
                    if hs:
                        load[min(hs, key=used) if even else hs[0]][0] += gr
                    else:
                        rest += gr
                for x in rest:
                    cs = [c for c in cw if used(c) < cap]
                    c = min(cs, key=lambda c: (c not in home[x[0]] and (x[0], c) not in cross, used(c)))
                    load[c][0].append(x)
                    if c not in home[x[0]]:
                        cross.add((x[0], c))
            for x in left:
                cs = [c for c in cores if used(c) < cap and load[c][0] and load[c][0][0][2] != 1]
                if not cs:
                    load = None
                    break
                c = min(cs, key=lambda c: (c not in home[x[0]] and (x[0], c) not in cross, not load[c][1], used(c)))
                load[c][1].append(x)
                if c not in home[x[0]]:
                    cross.add((x[0], c))
            if load is None:
                continue
            fan = max([sum(1 for p in cross if p[0] == r) for r in home])
            most = max(len(groups(a)) + len(groups(b)) for a, b in load.values())
            cost = (len(left), fan, len(cross), most, sum(used(c) for c in cores))
            if best is None or cost < best[0]:
                best = (cost, load)
    return best[1]


def place_near(off, on, c, h, cores):
    best = None
    for cfg in configs(2):
        width = {c: cfg[0], h: cfg[1]}
        out, stay, ok = {c: [], h: []}, {c: [], h: []}, True
        for todo, load in ((sorted(off, key=lambda x: x[2]), out), (sorted(on, key=lambda x: x[2]), stay)):
            while todo and ok:
                x = todo.pop()
                cs = [k for k in (c, h) if width[k] == x[2] and len(load[k]) < 8 and k != cores[x[3]]]
                if cs:
                    load[min(cs, key=lambda k: len(load[k]))].append(x)
                elif x[2] == 2:
                    todo = split(x) + todo
                else:
                    ok = False
        cost = sum(len(v) for v in out.values()) + sum(len(v) for v in stay.values())
        if ok and (best is None or cost < best[0]):
            best = (cost, out, stay)
    return best[1], best[2]


def schedule(cl, links):
    items = []
    for i, pools in enumerate(cl):
        for pool in (0, 1):
            items += [[i, gr, pool, len(gr)] for gr in groups(pools[pool])]
    ahead = lambda it: 128 * len(it[1]) // it[3] + LINK * max(links(u) for u in it[1])
    order = lambda i: sorted([it for it in items if it[0] == i], key=lambda it: -ahead(it))

    def score():
        t, worst, total = 0, 0, 0
        for i in range(len(cl)):
            for k, it in enumerate(order(i)):
                t += TRANSFER + (CALL if k == 0 else 0)
                worst = max(worst, t + ahead(it))
                total += t + ahead(it)
        return worst, total

    while True:
        tries = []
        for k, it in enumerate(items):
            if sum(o[3] for o in items if o[2] == it[2]) + it[3] <= 8:
                it[3] *= 2
                tries.append((score(), k))
                it[3] //= 2
        if not tries:
            break
        items[min(tries)[1]][3] *= 2
    at = [0, 8]
    out = []
    for i in range(len(cl)):
        trs = []
        for it in order(i):
            trs.append((it[1], ((1 << it[3]) - 1) << at[it[2]]))
            at[it[2]] += it[3]
        if trs:
            out.append(trs)
    return out


def plan(tables, cores, topo):
    route = tables["ROUTE"]
    n = len(cores)
    pos, fill = {}, [0] * n
    for r in range(n):
        for t in range(len(route[r])):
            for e in route[r][t]:
                pos[(r, t, e)] = fill[e]
                fill[e] += 1
    units = []
    for r in range(n):
        for e in range(n):
            ts = [t for t in range(len(route[r])) if e in route[r][t]]
            i = 0
            while i < len(ts):
                w = 2 if i + 1 < len(ts) and ts[i + 1] == ts[i] + 1 else 1
                units.append((r, ts[i], w, e))
                i += w
    chip = lambda r: topo.chip(cores[r])
    work = {}
    for ch in sorted(set(chip(r) for r in range(n))):
        rs = [r for r in range(n) if chip(r) == ch]
        far = [u for u in units if u[0] in rs and (chip(u[3]) & 1) != (ch & 1)]
        ports = [c for c in range(ch * 8, ch * 8 + 8) if c % 4 >= 2]
        home = {r: [c for c in ports if topo.die(c) == topo.die(cores[r])] for r in rs}
        for c, (one, two) in place_far(far, ports, home, lambda u: topo.mates(ch, chip(u[3]))).items():
            work[c] = [(one, []), (two, [])]
        for r in rs:
            off = [u for u in units if u[0] == r and chip(u[3]) != ch and (chip(u[3]) & 1) == (ch & 1)]
            on = [u for u in units if u[0] == r and chip(u[3]) == ch]
            out, stay = place_near(off, on, cores[r], cores[r] + 1, cores)
            for c in out:
                work[c] = [(out[c], stay[c])]

    def links(u):
        a, b = chip(u[0]), chip(u[3])
        return 0 if a == b else 1 if topo.mates(a, b) or topo.same_plane(a, b) else 2

    calls, feeds = {}, {cores[r]: [] for r in range(n)}
    for c, cl in work.items():
        calls[c] = []
        for trs in schedule(cl, links):
            calls[c].append([((cores[gr[0][0]] % 8) * 2 + gr[0][1], gr[0][2],
                              [(cores[u[3]], pos[(u[0], u[1], u[3])]) for u in gr], m) for gr, m in trs])
            for gr, m in trs:
                src = cores[gr[0][0]]
                if c != src and c not in feeds[src]:
                    feeds[src].append(c)
    return calls, feeds, fill


def rank_program(g, core, T, topo):
    calls, feeds, fill = plan(T.tables, T.cores, topo)
    rank = T.rank_of(core)

    def dst(c):
        return bass.DstId(rid=topo.addr(c)[0], pnc=topo.addr(c)[1])

    def send():
        left = 0
        for trs in calls.get(core, []):
            g.remote_dma_fused([bass.RemoteDMATransfer(dst_ids=[dst(d) for d, p in ds], dma_engine_mask=m,
                                                       remote_sem=T.sem.done, srcs=[T.xs[:, a:a + w]],
                                                       dsts=[T.land[:, p:p + w] for d, p in ds])
                                for (a, w, ds, m) in trs], local_sem=T.sem.done)
            left += sum(ones(m) for (a, w, ds, m) in trs)
        return left

    if rank is None:
        fed = sum(core in hs for hs in feeds.values())
        if fed:
            g.wait_ge(T.sem.got, 16 * fed)
            g.wait_ge(T.sem.done, send())
        return

    a = (core % 8) * 2
    g.dma_start(out=T.xs[:, a:a + 8], in_=T.x[:, :]).then_inc(T.sem.loaded, 16)
    g.wait_ge(T.sem.loaded, 16)
    hs = sorted(feeds[core], key=lambda h: h % 4 < 2)
    g.remote_dma_fused([bass.RemoteDMATransfer(dst_ids=[dst(h) for h in hs], dma_engine_mask=0xFFFF,
                                               remote_sem=T.sem.got, srcs=[T.xs[:, a:a + 8]],
                                               dsts=[T.xs[:, a:a + 8] for h in hs])], local_sem=T.sem.done)
    total = 16 + send()
    for cl in calls.values():
        for trs in cl:
            total += sum(ones(m) for (a2, w, ds, m) in trs for d, p in ds if d == core)
    g.wait_ge(T.sem.done, total)
    k = fill[rank]
    g.dma_start(out=T.y[:, 0:k], in_=T.land[:, 0:k]).then_inc(T.sem.stored, 16)
    g.wait_ge(T.sem.stored, 16)
